import numpy as np, ml_dtypes
CORES = [6,15,38,47]
N = 4
BF = ml_dtypes.bfloat16
def gentries(a):
    return np.ascontiguousarray(a.reshape(8, 16, -1).transpose(0, 2, 1)).reshape(8, -1)
def gtable(e):
    e = np.asarray(e); return np.ascontiguousarray(e.reshape(8, -1, 16).transpose(0, 2, 1)).reshape(128, -1).astype(np.int32)
W, I, J, A, B, P, RO = 4096, 2048, 1536, 8, 8, 128, 4
def column(i, j):
    return ((((2 * i + 1) * (2 * j + 1)) >> 5) + 37 * i + j) & (W - 1)
def sized(rng, n, lo, hi, noise):
    b = np.exp2(lo + (hi - lo) * rng.random((N, 8, 1, n), dtype=np.float32))
    return (b * np.exp2(noise * (2 * rng.random((N, 8, 16, n), dtype=np.float32) - 1))).astype(np.int64)
def parts(rng):
    v = np.minimum(np.maximum(sized(rng, W, 2.6, 6.8, 0.5), 1), 127)
    rl = rng.integers(0, J, (N, 8, 16, I)); cl = rng.integers(0, I, (N, 8, 16, J))
    i = rng.integers(0, I, (N, 8, P)); j = rng.integers(0, J, (N, 8, P))
    return v, rl, cl, i, j, np.minimum(sized(rng, P, 1.0, 6.0, 0.5), 127)
def pack(v, rl, cl, i, j, z):
    return {"fig": np.ascontiguousarray(v.reshape(N, 128, W)).astype(np.float32).astype(BF), "rmate": np.ascontiguousarray(rl.reshape(N, 128, I)).astype(np.int32), "cmate": np.ascontiguousarray(cl.reshape(N, 128, J)).astype(np.int32),
            "prow": np.stack([gtable(a) for a in i]), "pcol": np.stack([gtable(a) for a in j]), "need": np.ascontiguousarray(z.reshape(N, 128, P)).astype(np.float32).astype(BF)}
def some(rng, good, free):
    n = np.flatnonzero(good & free)
    if len(n) == 0: n = np.flatnonzero(free)
    return n[rng.integers(0, len(n), 128)]
def fill(rng, v, rl, cl, i, j, z, g):
    v[:, g] = 40 + np.argsort(rng.random((N, 16, W)), axis=1); z[:, g] = 0
    seen = np.zeros((N, W), bool); rows = np.zeros((N, I), bool); cols = np.zeros((N, J), bool); ai = np.arange(I); aj = np.arange(J)
    for q in range(N):
        i[q, g] = rng.permutation(I)[:P]; j[q, g] = rng.permutation(J)[:P]; rows[q, i[q, g]] = True; cols[q, j[q, g]] = True
    x = np.array(i[:, g]); y = np.array(j[:, g])
    for t in range(RO):
        if t == RO - 1: rows[:] = False; cols[:] = False
        nx = np.zeros_like(x); ny = np.zeros_like(y)
        for q in range(N):
            to = (q + 1 + t % 3) % N
            for k in range(P):
                a, b = int(x[q, k]), int(y[q, k])
                u = some(rng, ~seen[q][column(a, aj)], ~cols[to]); w = some(rng, ~seen[q][column(ai, b)], ~rows[to])
                c = np.stack([column(a, u), column(w, b), column(w, u)])
                n = int(np.argmax(~seen[q][c[2]] & (c[0] != c[1]) & (c[0] != c[2]) & (c[1] != c[2])))
                seen[q, c[:, n]] = True; cols[to, u[n]] = True; rows[to, w[n]] = True
                rl[q, g, :, a] = u[n]; cl[q, g, :, b] = w[n]; nx[to, k] = w[n]; ny[to, k] = u[n]
        x, y = nx, ny
def setup_inputs(rng):
    return pack(*parts(rng))
def setup_inputs_ties(rng):
    v, rl, cl, i, j, z = parts(rng)
    v = rng.choice(np.array([8, 16, 32, 64]), (N, 8, 1, W)) + np.zeros((1, 1, 16, 1), np.int64)
    low = (rng.random((N, 8, 1, W)) < 0.3) & (np.arange(16)[:, None] == rng.integers(0, 16, (N, 8, 1, W)))
    z = rng.choice(np.array([0, 1, 8, 9, 16, 32, 33, 64, 65]), (N, 8, 1, P)) + np.zeros((1, 1, 16, 1), np.int64)
    v = v - low; fill(rng, v, rl, cl, i, j, z, 3)
    return pack(v, rl, cl, i, j, z)
def setup_inputs_none(rng):
    v, rl, cl, i, j, z = parts(rng)
    h = int(rng.integers(0, 8)); z[int(rng.integers(0, N))] = 0; z[:, h] = 127; v[:, h] = np.minimum(v[:, h], 126)
    for g, a, b in (((h + 1) % 8, A - 1, B - 1), ((h + 2) % 8, 0, 0)):
        v[:, g] = np.minimum(v[:, g], 10); z[:, g] = rng.integers(20, 30, (N, 16, P))
        for q in range(N):
            for k in range(8):
                x, y = int(i[q, g, k]), int(j[q, g, k]); u, w = int(rl[q, g, a, x]), int(cl[q, g, b, y])
                for c in (column(x, u), column(w, y), column(w, u)): v[q, g, :, c] = 127
    return pack(v, rl, cl, i, j, z)
def setup_inputs_alike(rng):
    v, rl, cl, i, j, z = parts(rng); z = z // 4
    i[:, [0, 4]] = i[:, [0, 4], :1]; j[:, [0, 4]] = j[:, [0, 4], :1]; z[:, [0, 4]] = z[:, [0, 4], :, :1]
    rl[:, [1, 5]] = rng.choice(np.array([0, 5, J - 1]), (N, 2, 16, I)); cl[:, [1, 5]] = rng.choice(np.array([0, 7, I - 1]), (N, 2, 16, J))
    i[:, 2] = rng.choice(np.array([0, 1, I // 2, I - 1]), (N, P)); j[:, 2] = rng.choice(np.array([0, 1, J // 2, J - 1]), (N, P))
    rl[:, 6] = rl[:, 6, :1]; cl[:, 6] = cl[:, 6, :1]
    for q in range(N):
        rl[q, 7, 0, i[q, 7]] = j[q, 7]; cl[q, 7, 0, j[q, 7]] = i[q, 7]
        cl[q, 4, :, int(j[q, 4, 0])] = int(i[q, 4, 0])
    z[:, 4] = 0
    rl[:, 3] = np.where(rng.random((N, 16, I)) < 0.5, rng.choice(np.array([0, J - 1]), (N, 16, I)), rl[:, 3])
    cl[:, 3] = np.where(rng.random((N, 16, J)) < 0.5, rng.choice(np.array([0, I - 1]), (N, 16, J)), cl[:, 3])
    i[:, 3] = np.where(rng.random((N, P)) < 0.5, rng.choice(np.array([0, I - 1]), (N, P)), i[:, 3])
    j[:, 3] = np.where(rng.random((N, P)) < 0.5, rng.choice(np.array([0, J - 1]), (N, P)), j[:, 3])
    return pack(v, rl, cl, i, j, z)
def setup_inputs_late(rng):
    v, rl, cl, i, j, z = parts(rng); z = z // 4
    for g in range(8):
        s = rng.permutation(16)
        for q in range(N):
            a, b = int(s[q % 2]), int(s[1 - q % 2])
            v[q, g, a] = np.minimum(v[q, g, a], 12); z[q, g, a] = rng.integers(13, 30, P); z[q, g, b] = np.minimum(z[q, g, b], 6)
    return pack(v, rl, cl, i, j, z)
def setup_inputs_spread(rng):
    v, rl, cl, i, j, z = parts(rng)
    v = np.minimum(np.maximum(sized(rng, W, 0.0, 7.3, 0.3), 1), 127)
    z = np.minimum(sized(rng, P, -1.0, 7.2, 0.2), 127)
    v[:, 2] = rng.integers(123, 128, (N, 16, W)); z[:, 2] = np.minimum(z[:, 2], 60)
    v[:, 5] = np.where(rng.random((N, 1, W)) < 0.5, 127, 1); z[:, 5] = 127
    return pack(v, rl, cl, i, j, z)
def check_inputs(d):
    bad = []
    for k, lo, hi in (("fig", 1, 127), ("rmate", 0, J - 1), ("cmate", 0, I - 1), ("prow", 0, I - 1), ("pcol", 0, J - 1), ("need", 0, 127)):
        v = np.asarray(d[k]).astype(np.float64)
        if not (np.all(v >= lo) and np.all(v <= hi) and np.all(v == np.floor(v))): bad.append("range of " + k)
    return bad
def look(h, c, z):
    m = c.shape[1]; v = np.take_along_axis(h, c.reshape(8, 1, m * P), 2).reshape(8, 16, m, P)
    return np.all(np.abs(v) >= z[:, :, None, :], axis=1), np.sum(np.maximum(v, 0), axis=1)
def reference(fig, rmate, cmate, prow, pcol, need):
    h = fig.astype(np.float32).astype(np.int32).reshape(N, 8, 16, W); z = need.astype(np.float32).astype(np.int32).reshape(N, 8, 16, P)
    rm = rmate.astype(np.int64).reshape(N, 8, 16, I); cm = cmate.astype(np.int64).reshape(N, 8, 16, J)
    i = np.stack([gentries(a) for a in prow]).astype(np.int64); j = np.stack([gentries(a) for a in pcol]).astype(np.int64)
    cost = np.zeros((N, 8, RO, P), np.float32); gi = np.arange(8)[:, None] + np.zeros((1, P), np.int64)
    for t in range(RO):
        ra = A * (t % (16 // A)); rb = B * (t % (16 // B)); sh = 1 + t % 3
        ni, nj, nz = [None] * N, [None] * N, [None] * N
        for q in range(N):
            x, y = i[q], j[q]
            jm = np.take_along_axis(rm[q][:, ra:ra + A], x[:, None, :], 2)
            im = np.take_along_axis(cm[q][:, rb:rb + B], y[:, None, :], 2)
            ok1, c1 = look(h[q], column(x[:, None, :], jm), z[q]); ok2, c2 = look(h[q], column(im, y[:, None, :]), z[q])
            ok3, c3 = look(h[q], column(im[:, None, :, :], jm[:, :, None, :]).reshape(8, A * B, P), z[q])
            ok = (ok1[:, :, None, :] & ok2[:, None, :, :]).reshape(8, A * B, P) & ok3
            total = (c1[:, :, None, :] + c2[:, None, :, :]).reshape(8, A * B, P) + c3
            total = np.where(ok, total, 2 ** 20)
            best = np.argmin(total, axis=1); good = np.any(ok, axis=1)
            cost[q, :, t] = np.where(good, np.take_along_axis(total, best[:, None, :], 1)[:, 0], -1)
            u = np.take_along_axis(jm, (best // B)[:, None, :], 1)[:, 0]; w = np.take_along_axis(im, (best % B)[:, None, :], 1)[:, 0]
            far = column(w, u); hit = np.zeros((8, W), bool)
            for c in (column(x, u), column(w, y), far): hit[gi[good], c[good]] = True
            size = np.abs(h[q]); fresh = np.take_along_axis(size, far[:, None, :], 2) >> 1
            h[q] = np.where(hit[:, None, :], -size, h[q])
            to = (q + sh) % N
            ni[to] = np.where(good, w, x); nj[to] = np.where(good, u, y); nz[to] = np.where(good[:, None, :], fresh, z[q])
        i = np.stack(ni); j = np.stack(nj); z = np.stack(nz)
    yp = np.stack([gtable(np.concatenate([i[q], j[q]], axis=1)) for q in range(N)])
    return {"yf": h.reshape(N, 128, W).astype(np.float32).astype(BF), "yp": yp.astype(np.float32), "yz": z.reshape(N, 128, P).astype(np.float32).astype(BF), "yc": cost.reshape(N, 8, RO * P)}

from concourse.mybir import AluOpType as A, ActivationFunctionType as F

ROT = 315
W, NI, NJ = 4096, 2048, 1536
BAD = float(2 ** 20)
CLIP = float(2 ** 20 - 64)
PC = 17704.5
ROUNDS = 4
NS = [4, 4, 4, 6]
NSM = 6

SB = {}
POOL = {}
USED = {"poolF": 0, "poolI": 0}


def _sb(names, shape, dtype="float32"):
    for n in names.split():
        SB[n] = ("sbuf", [128] + shape, dtype)


def _small(names, width, dtype="float32"):
    p = "poolF" if dtype == "float32" else "poolI"
    for n in names.split():
        POOL[n] = (p, USED[p], width)
        USED[p] += width


_small("rhoI Pi far2 FC3", 8, "int32")
_small("KJ k0 k1 gn PP t8 kj P8 MB", 8)
_small("mki cI", 8 * ROUNDS, "int32")
_small("G cf cst", 8 * ROUNDS)
_small("XYi", 16, "int32")
_small("XYf UWO UWN T16 H16 PH YP", 16)
_small("QC", 24, "int32")
_small("HLi", 48, "int32")
_small("HLf", 48)
_small("SP SN", NSM)
_small("T32 MA", 32)
_small("M2", 64)
_small("PI P15i", 1, "int32")
_small("PF P15 G16 SLO SHI SCA BIA SCB BIB CWT CW2 PKC PM PMA QA QB QB8 QJ1 QJ2 QJ3", 1)
_sb("poolF", [USED["poolF"]])
_sb("poolI", [USED["poolI"]], "int32")
_sb("prowI pcolI", [8], "int32")
_sb("rhoU farU", [8], "uint16")
for _t in range(ROUNDS + 1):
    _sb("XY%d" % _t, [16], "uint16")
    _sb("Z%d" % _t, [128], "bfloat16")
_sb("XYs", [16], "uint16")
_sb("Zs", [128], "bfloat16")
_sb("XM0 XM1", [NI], "int32")
_sb("MW", [W + 128], "bfloat16")
_sb("CW YF", [W], "bfloat16")
_sb("IOTA", [NI])
_sb("ONE BT BB OFF C16 C8 CAL MI NPC", [128])
_sb("C16b IDb HIO", [128], "bfloat16")
_sb("sJ0 sJ1 sJ2 sJ3 sA sB sI PK IDf DMK", [128])
_sb("SEL SELC EXPM", [16, 128], "bfloat16")
_sb("RHO", [512], "bfloat16")
_sb("RST", [256])
_sb("M1", [512])
_sb("OHA OHB T64", [64])
_sb("OHW", [80])
_sb("LIO SG", [256], "bfloat16")
_sb("R2 C2 U WN OT IPs MT2s NM NMm", [128])
_sb("K2Y", [8, 16])
_sb("K1s", [4, 8, 2])
_sb("F12q F12i", [128], "int32")
_sb("F12u", [128], "uint16")
_sb("F3q F3i", [512], "int32")
_sb("F3u", [512], "uint16")
_sb("Zr E12v E12c", [2048], "bfloat16")
_sb("E3v E3c", [8192], "bfloat16")
_sb("HOH", [24, 128], "bfloat16")
_sb("LOH", [24, 256], "bfloat16")
_sb("ST1 ST2", [NSM, 256], "bfloat16")
_sb("CSi HCi LCi", [256], "int32")
_sb("HLC", [2, 256], "bfloat16")
_sb("YZ", [128], "bfloat16")
for _n in ("pJP", "pM", "pM2", "pA", "pB", "pN", "pH"):
    SB[_n] = ("psum", [128, 512], "float32")
SB["pK"] = ("psum", [128, 8, 16], "float32")
PSUMS = ("pJP", "pM", "pM2", "pA", "pB", "pN", "pH", "pK")
SCRATCH = SB
NDMA = 60
SEMAPHORES = ["qv", "qt", "qs", "qg"] + ["d%d" % k for k in range(NDMA)] + \
    [p + "%d" % k for p in ("rn", "rz", "ln", "lz") for k in range(ROUNDS)]


def rank_program(g, core, T, topo):
    rank = T.rank_of(core)
    if rank is None:
        return
    queues = {"v": g.vector, "t": g.tensor, "s": g.scalar, "g": g, "y": g.sync}
    count = {}
    known = {q: {} for q in queues}
    past = {}
    ndma = [0]

    def need_waits(q, reads, writes, is_dma):
        deps = []
        for regs, w in ((reads, False), (writes, True)):
            for (n, lo, hi) in regs:
                bank = n in PSUMS
                for (plo, phi, pw, pq, sem, val, kn) in past.get(n, ()):
                    same = pq == q and not is_dma
                    if bank:
                        if same and not (pw or w):
                            continue
                    elif phi <= lo or plo >= hi or not (pw or w):
                        continue
                    if same and (q == "t" or not pw):
                        continue
                    deps.append((sem, val, kn))
        for sem, val, kn in sorted(deps, key=lambda d: -d[1]):
            if known[q].get(sem, 0) < val:
                queues[q].wait_ge(T.sem[sem], val)
                known[q][sem] = val
                for s2, v2 in kn.items():
                    if known[q].get(s2, 0) < v2:
                        known[q][s2] = v2

    def note(q, sem, val, reads, writes, kn):
        for regs, w in ((reads, False), (writes, True)):
            for (n, lo, hi) in regs:
                lst = past.setdefault(n, [])
                if n in PSUMS:
                    lst[:] = [p for p in lst if not (p[3] == q and (w or not p[2]) and lo <= p[0] and p[1] <= hi)]
                elif w:
                    lst[:] = [p for p in lst if not (lo <= p[0] and p[1] <= hi)]
                lst.append((lo, hi, w, q, sem, val, kn))

    def regs_of(*refs):
        out = []
        for r in refs:
            if isinstance(r, tuple):
                out += r[1]
        return out

    def emit(q, call, reads, writes):
        sem = "q" + q
        need_waits(q, reads, writes, False)
        inst = call()
        count[sem] = count.get(sem, 0) + 1
        inst.then_inc(T.sem[sem], 1)
        note(q, sem, count[sem], reads, writes, dict(known[q]))

    def dma(q, out, in_):
        sem = "d%d" % ndma[0]
        ndma[0] += 1
        need_waits(q, in_[1], out[1], True)
        queues[q].dma_start(out[0], in_[0]).then_inc(T.sem[sem], 16)
        count[sem] = 16
        note(sem, sem, 16, in_[1], out[1], dict(known[q]))

    def R(n, lo=0, hi=None, step=1):
        if n in POOL:
            p, base, width = POOL[n]
            hi = width if hi is None else hi
            n, lo, hi = p, base + lo, base + hi
        elif hi is None:
            hi = SB[n][1][1]
        return (T[n][:, lo:hi:step] if step > 1 else T[n][:, lo:hi], [(n, lo, hi)])

    def X(ap, n, lo=0, hi=1 << 20):
        return (ap, [(n, lo, hi)])

    def IND(win, offs):
        return (win[0].indirect(offs[0]), win[1] + offs[1])

    def val(x):
        return x[0] if isinstance(x, tuple) else x

    def TT(out, a, b, op):
        emit("v", lambda: g.vector.tensor_tensor(out[0], a[0], b[0], op), regs_of(a, b), out[1])

    def TS(out, a, s1, s2, op0, op1=None):
        if op1 is None:
            emit("v", lambda: g.vector.tensor_scalar(out[0], a[0], val(s1), None, op0), regs_of(a, s1), out[1])
        else:
            emit("v", lambda: g.vector.tensor_scalar(out[0], a[0], val(s1), val(s2), op0, op1), regs_of(a, s1, s2), out[1])

    def TC(out, a):
        emit("v", lambda: g.vector.tensor_copy(out[0], a[0]), regs_of(a), out[1])

    def MS(out, c):
        emit("v", lambda: g.vector.memset(out[0], c), [], out[1])

    def SCAN(out, d0, d1, init, op0, op1):
        emit("v", lambda: g.vector.tensor_tensor_scan(out[0], d0[0], d1[0], init, op0, op1), regs_of(d0, d1), out[1])

    def ACT(out, a, func, bias=0.0, scale=1.0):
        emit("s", lambda: g.scalar.activation(out[0], a[0], func, bias=val(bias), scale=val(scale)), regs_of(a, bias, scale), out[1])

    def MM(out, pairs, start=True, stop=True):
        def go():
            inst = None
            for k, (l, r) in enumerate(pairs):
                inst = g.tensor.matmul(out[0], l[0], r[0], start and k == 0, stop and k == len(pairs) - 1)
            return inst
        emit("t", go, regs_of(*[r for p in pairs for r in p]), out[1])

    def IOTA(out, pattern, base, cm, f=True):
        if f:
            emit("g", lambda: g.iota(out[0], pattern, base, cm, allow_small_or_imprecise_dtypes=True), [], out[1])
        else:
            emit("g", lambda: g.iota(out[0], pattern, base, cm), [], out[1])

    def AFF(out, in_, pattern, op, fill, base, cm):
        emit("g", lambda: g.affine_select(out[0], in_[0], pattern, op, fill, base, cm), in_[1], out[1])

    def remote(t, kind, dst, src):
        sh = 1 + t % 3
        to = T.cores[(rank + sh) % 4]
        rid, pid, _ = topo.addr(to)
        ls, rs = "l%s%d" % (kind, t), "r%s%d" % (kind, t)
        need_waits("g", src[1], [], True)
        g.remote_dma(T[dst][:], src[0], T.sem[rs], T.sem[ls], pid, rid, topo.mask(core, to))
        count[ls] = len(topo.engines(core, to))
        note(ls, ls, count[ls], src[1], [], dict(known["g"]))
        frm = T.cores[(rank - sh) % 4]
        count[rs] = len(topo.engines(frm, core))
        note(rs, rs, count[rs], [], [(dst, 0, SB[dst][1][1])], {})

    eq, ge, SHR, AND = A.is_equal, A.is_ge, A.arith_shift_right, A.bitwise_and
    EXT = []

    def mates(h, qs):
        n = "XM%d" % h
        for k in range(8):
            dma(qs[k % 2], X(T[n][16 * k:16 * k + 8, 0:NI], n, k, k + 1), (T.rmate[16 * k + 8 * h:16 * k + 8 * h + 8, :], EXT))
        for k in range(8):
            dma(qs[k % 2], X(T[n][16 * k + 8:16 * k + 16, 0:NJ], n, 8 + k, 9 + k), (T.cmate[16 * k + 8 * h:16 * k + 8 * h + 8, :], EXT))
    dma("y", R("prowI"), (T.prow[:], EXT))
    dma("s", R("pcolI"), (T.pcol[:], EXT))
    dma("y", R("MW", ROT, W), (T.fig[:, 0:W - ROT], EXT))
    dma("s", R("MW", 0, ROT), (T.fig[:, W - ROT:W], EXT))
    MS(X(T.XM0[:, NJ:NI], "XM0"), 0)
    mates(0, "ys")
    dma("s", R("Z0"), (T.need[:], EXT))

    MS(R("ONE"), 1.0)
    MS(R("CW"), 0.0)
    IOTA(R("PI"), [[1, 1]], 0, 1, False)
    AFF(R("BT"), R("ONE"), [[-16, 8], [0, 16]], ge, 0.0, 0, 1)
    AFF(R("BB"), R("BT"), [[16, 8], [0, 16]], ge, 0.0, 15, -1)
    IOTA(R("C16"), [[0, 8], [1, 16]], 0, 0)
    IOTA(R("C8"), [[0, 16], [1, 8]], 0, 0)
    IOTA(R("CAL"), [[0, 8], [1, 2], [0, 8]], 0, 0)
    IOTA(R("IOTA"), [[1, NI]], 0, 0)
    IOTA(R("MI"), [[1, 128]], 0, 0)
    IOTA(R("LIO"), [[1, 256]], 0, 0)
    IOTA(R("RHO"), [[16, 4], [0, 8], [1, 16]], 0, 0)
    IOTA(R("OHA"), [[1, 8], [0, 8]], 0, 0)
    IOTA(R("OHB"), [[0, 8], [1, 8]], 8, 0)
    IOTA(R("DMK"), [[1, 8], [0, 8], [8, 2]], 0, 0)
    IOTA(R("KJ"), [[16, 8]], W, 0)
    IOTA(R("H16"), [[1, 16]], 0, 0)
    IOTA(R("RST"), [[0, 32], [1, 8]], 0, 0)

    TS(R("P15i"), R("PI"), 15, None, AND)
    TC(R("PF"), R("PI"))
    TC(R("P15"), R("P15i"))
    TS(R("OFF"), R("BB"), -999.0, 999.0, A.mult, A.add)
    TT(R("C16"), R("C16"), R("OFF"), A.add)
    TC(R("C16b"), R("C16"))
    for c in range(16):
        TS(X(T.SEL[:, c, :], "SEL", c, c + 1), R("C16b"), float(c), BAD, eq, A.mult)
    TS(R("SLO"), R("P15"), 8.0, None, A.is_lt)
    TS(R("SHI"), R("P15"), 8.0, None, ge)
    TS(R("SCA"), R("SLO"), 2.0, None, A.mult)
    TS(R("BIA"), R("SLO"), 17.0, None, A.mult)
    TS(R("SCB"), R("SHI"), 2.0, None, A.mult)
    TS(R("BIB"), R("SHI"), 593.0, None, A.mult)
    TS(R("PM"), R("SHI"), -50.0, None, A.mult)
    TT(R("QA"), R("P15"), R("PM"), A.add)
    TS(R("PMA"), R("SLO"), -50.0, -8.0, A.mult, A.add)
    TT(R("QB"), R("P15"), R("PMA"), A.add)
    TS(R("QB8"), R("QB"), 8.0, None, A.add)
    for a in range(1, 4):
        TS(R("QJ%d" % a), R("QA"), -2.0 * a, None, A.add)
    for n in ("C8", "CAL"):
        TT(R(n), R(n), R("OFF"), A.add)
    TS(R("sA"), R("C16"), R("QA"), None, eq)
    TS(R("sB"), R("C16"), R("QB8"), None, eq)
    TS(R("sI"), R("C8"), R("QB"), None, eq)
    for a in range(4):
        TS(R("sJ%d" % a), R("CAL"), R("QJ%d" % a if a else "QA"), None, eq)
    TC(R("XY0", 0, 8), R("prowI"))
    TC(R("XY0", 8, 16), R("pcolI"))

    def sums():
        for h in range(16):
            MM(R("pH", 0, 256), [(X(T.SEL[:, h, :], "SEL", h, h + 1), R("MW", 256 * h, 256 * h + 256))], h == 0, h == 15)
        TS(R("CSi"), R("pH", 0, 256), 1.0 / BAD, None, A.mult)
        TS(R("HCi"), R("CSi"), 4, None, SHR)
        TS(R("LCi"), R("CSi"), 15, None, AND)
        TC(X(T.HLC[:, 0, :], "HLC", 0, 256), R("HCi"))
        TC(X(T.HLC[:, 1, :], "HLC", 256, 512), R("LCi"))

    def spread_sums():
        for k in range(2):
            dma("y", X(T.CW[k::16, :], "CW", k, k + 1), X(T.HLC[:, k, :], "HLC", 256 * k, 256 * k + 256))

    sums()
    spread_sums()
    MS(X(T.XM1[:, NJ:NI], "XM1"), 0)
    mates(1, "yy")
    MS(R("OHW"), 0.0)
    MS(R("NPC"), -PC)
    TS(R("CWT"), R("P15"), 0.0, 2048.0 / BAD, eq, A.mult)
    TS(R("CW2"), R("P15"), 1.0, 128.0 / BAD, eq, A.mult)
    TT(R("CWT"), R("CWT"), R("CW2"), A.add)
    TS(X(T.SELC[:], "SELC"), X(T.SEL[:], "SEL"), R("CWT"), None, A.mult)
    TS(R("IDb"), R("MI"), R("PF"), None, eq)
    TS(R("IDf"), R("MI"), R("PF"), None, eq)

    def late_constants():
        TS(R("PKC"), R("SHI"), 1023.5, 0.5, A.mult, A.add)
        TS(R("PK"), R("BB"), R("PKC"), None, A.mult)
        TS(R("RST"), R("RST"), 0.0, 1e9, eq, A.mult)
        TS(R("OHA"), R("OHA"), R("P15"), None, eq)
        TS(R("OHB"), R("OHB"), R("P15"), None, eq)
        TT(R("OHW", 0, 64), R("OHA"), R("OHB"), A.add)
        TS(R("DMK"), R("DMK"), R("P15"), None, eq)
        TS(R("KJ"), R("KJ"), R("P15"), None, A.add)
        TT(R("G16"), R("PF"), R("P15"), A.subtract)
        TS(R("HIO"), R("MI"), R("G16"), None, A.subtract)
        TS(R("PH"), R("H16"), R("P15"), None, eq)
        for c in range(16):
            TS(X(T.EXPM[:, c, :], "EXPM", c, c + 1), R("BB"), R("PH", c, c + 1), None, A.mult)

    def suppress(ns):
        first = 24 - ns
        TS(R("SP", 0, ns), R("HLf", 24 + first, 48), -1.0, 0.5, A.mult, A.add)
        TS(R("SN", 0, ns), R("HLf", 24 + first, 48), 0.5, None, A.add)
        for k in range(ns):
            ACT(X(T.ST1[:, k, :], "ST1", k, k + 1), R("LIO"), F.Sign, bias=R("SP", k, k + 1))
            ACT(X(T.ST2[:, k, :], "ST2", k, k + 1), R("LIO"), F.Sign, bias=R("SN", k, k + 1), scale=-1.0)
        order = list(range(0, 10)) + list(range(first, 24)) + list(range(10, first))
        for n, e in enumerate(order):
            hoh = X(T.HOH[:, e, :], "HOH", e, e + 1)
            TS(hoh, R("HIO"), R("HLf", e, e + 1), R("gn", e % 8, e % 8 + 1), eq, A.mult)
            if e < first:
                loh = X(T.LOH[:, e, :], "LOH", e, e + 1)
                TS(loh, R("LIO"), R("HLf", 24 + e, 25 + e), 2.0, eq, A.mult)
                MM(R("pH", 0, 256), [(hoh, loh)], n == 0, n == 23)
            else:
                k = e - first
                MM(R("pH", 0, 256), [(hoh, X(T.ST1[:, k, :], "ST1", k, k + 1)), (hoh, X(T.ST2[:, k, :], "ST2", k, k + 1))], False, n == 23)

    for t in range(ROUNDS):
        xy, z = "XY%d" % t, "Z%d" % t
        zoff = 0.0 if t == 0 else -128.0
        LX, LY = R(xy, 0, 8), R(xy, 8, 16)
        XM = R("XM%d" % (t % 2))
        TS(R("R2"), IND(XM, LX), 2.0, 593.0, A.mult, A.add)
        ACT(R("U"), IND(R("IOTA"), LX), F.Identity, bias=R("BIA"), scale=R("SCA"))
        ACT(R("WN"), IND(R("IOTA"), LY), F.Identity, bias=R("BIB"), scale=R("SCB"))
        TS(R("C2"), IND(XM, LY), 2.0, 17.0, A.mult, A.add)
        if t:
            for k in range(2):
                hl = X(T.HLC[:, k, :], "HLC", 256 * k, 256 * k + 256)
                TT(hl, hl, R("pH", 0, 256), A.subtract)
            spread_sums()
        MM(R("pM", 0, 128), [(R("sA"), R("R2"))], True, False)
        MM(R("pM", 0, 128), [(R("sB"), R("C2"))], False, True)
        MM(R("pN", 0, 128), [(R("sI"), R("C2"))])
        JP = [R(("pJP", "pA")[a // 2], 128 * (a % 2), 128 * (a % 2) + 128) for a in range(4)]
        for a in range(4):
            MM(JP[a], [(R("sJ%d" % a), R("R2"))])
        for k in range(16):
            if k == 12:
                ACT(R("IPs"), R("pN", 0, 128), F.Copy)
            ACT(X(T.Zr[:, k:2048:16], "Zr", k, k + 1), R(z), F.Copy, bias=zoff)
        ACT(X(T.MW[:, W:W + 128], "MW", W, W + 128), R(z), F.Copy, bias=2 * zoff, scale=2.0)
        TT(R("OT"), R("U"), R("WN"), A.add)
        TC(R("XYf"), R(xy))
        TS(R("UWO", 0, 8), R("XYf", 0, 8), 2.0, 17.0, A.mult, A.add)
        TS(R("UWO", 8, 16), R("XYf", 8, 16), 2.0, 593.0, A.mult, A.add)
        TS(R("t8"), R("XYf", 0, 8), 2048.0, PC, A.mult, A.add)
        TT(R("PP"), R("t8"), R("XYf", 8, 16), A.add)
        TT(R("F12q"), R("pM", 0, 128), R("OT"), A.mult)
        TS(R("F12i"), R("F12q"), 5, W - 1, SHR, AND)
        TC(R("F12u"), R("F12i"))
        for a in range(4):
            TT(R("F3q", 128 * a, 128 * a + 128), JP[a], R("IPs"), A.mult)
        TS(R("F3i"), R("F3q"), 5, W - 1, SHR, AND)
        TC(R("F3u"), R("F3i"))

        def look_v(e, lo, f, flo, n):
            TT(R(e, lo, lo + 16 * n), IND(R("MW", 0, W), R(f, flo, flo + n)), X(T.Zr[:, lo % 2048:lo % 2048 + 16 * n], "Zr"), A.is_lt)

        def look_c(e, lo, f, flo, n):
            ACT(R(e, lo, lo + 16 * n), IND(R("CW"), R(f, flo, flo + n)), F.Relu)

        def chunk(out, e, off, sel, start, stop, c0=0, c1=16):
            for c in range(c0, c1):
                MM(out, [(X(T[sel][:, c, :], sel, c, c + 1), R(e, off + 128 * c, off + 128 * c + 128))], start and c == 0, stop and c == 15)
        PKR = X(T.pK[:], "pK")
        look_c("E12c", 0, "F12u", 0, 128)
        look_v("E12v", 0, "F12u", 0, 128)
        for b, nm in enumerate(("pA", "pB")):
            MM(R(nm, 0, 256), [(R("IDb"), R("RHO", 256 * b, 256 * b + 256))], True, False)
        for k in range(8):
            MM(R("pM2", 16 * k, 16 * k + 16), [(R("sA"), R("R2", k, 128, 8)), (R("sB"), R("C2", k, 128, 8))])
        chunk(PKR, "E12v", 0, "SEL", True, False)
        banks = [R(("pA", "pB")[a // 2], 128 * (a % 2), 128 * (a % 2) + 128) for a in range(4)]
        for a in range(4):
            lo = 2048 * a
            parts = ((0, 128),) if a < 3 else ((0, 64), (64, 32), (96, 32))
            for (p, n) in parts:
                look_v("E3v", lo + 16 * p, "F3u", 128 * a + p, n)
                look_c("E3c", lo + 16 * p, "F3u", 128 * a + p, n)
            if a == 0:
                chunk(PKR, "E12c", 0, "SELC", False, True)
                if t == 0:
                    late_constants()
            if a == 1:
                ACT(R("MT2s"), R("pM2", 0, 128), F.Copy)
                for l in range(2):
                    ACT(X(T.K2Y[:, :, 8 * l:8 * l + 8], "K2Y", l, l + 1), X(T.pK[:, :, 8:16], "pK"), F.Copy)
                for x in range(4):
                    ACT(X(T.K1s[:, x, :, :], "K1s", x, x + 1), X(T.pK[:, :, 2 * x:2 * x + 2], "pK"), F.Copy)
                for x in range(2):
                    MM(banks[x], [(R("IDf"), X(T.K2Y[:], "K2Y"))], False, False)
            if a == 2:
                for x in range(2):
                    MM(banks[2 + x], [(R("IDf"), X(T.K2Y[:], "K2Y"))], False, False)
                MM(R("pN", 0, 128), [(R("IDf"), R("NPC"))], True, False)
            for (p, n) in parts:
                chunk(banks[a], "E3c", lo, "SELC", False, False, p // 8, (p + n) // 8)
                chunk(banks[a], "E3v", lo, "SEL", False, a % 2 == 1, p // 8, (p + n) // 8)
        for b, nm in enumerate(("pA", "pB")):
            SCAN(R("M1", 256 * b, 256 * b + 256), R("RST"), R(nm, 0, 256), 0.0, A.max, A.min)
            m = R("M2", 32 * b, 32 * b + 32)
            TT(m, R("M1", 256 * b + 7, 256 * b + 256, 8), X(T.K1s[:, 2 * b:2 * b + 2, :, :], "K1s", 2 * b, 2 * b + 2), A.add)
            TT(R("MA", 16 * b, 16 * b + 16), R("M2", 32 * b, 32 * b + 16), R("M2", 32 * b + 16, 32 * b + 32), A.min)
        TT(R("MA", 0, 16), R("MA", 0, 16), R("MA", 16, 32), A.min)
        TT(R("MB"), R("MA", 0, 16, 2), R("MA", 1, 16, 2), A.min)
        mk = R("mki", 8 * t, 8 * t + 8)
        TS(mk, R("MB"), CLIP, None, A.min)
        TS(R("rhoI"), mk, 127, None, AND)
        TC(R("rhoU"), R("rhoI"))
        TT(R("NM"), IND(R("OHW"), R("rhoU")), R("MT2s"), A.mult)
        MM(R("pN", 0, 128), [(R("PK"), R("NM"))], False, True)
        if t == ROUNDS - 1:
            TS(R("cI"), R("mki"), 7, None, SHR)
            TS(R("G"), R("mki"), CLIP, None, A.is_lt)
            TS(R("cf"), R("cI"), 1.0, None, A.add)
        TT(R("NMm"), R("pN", 0, 128), R("DMK"), A.mult)
        TT(R("T64"), R("NMm", 0, 64), R("NMm", 64, 128), A.add)
        TT(R("T32"), R("T64", 0, 32), R("T64", 32, 64), A.add)
        TT(R("T16"), R("T32", 0, 16), R("T32", 16, 32), A.add)
        TT(R("P8"), R("T16", 0, 16, 2), R("T16", 1, 16, 2), A.add)
        TS(R("k0"), R("P8"), 0.0, None, A.is_lt)
        TT(R("k1"), R("k0"), R("PP"), A.mult)
        TT(R("Pi"), R("P8"), R("k1"), A.add)
        TS(R("XYi", 0, 8), R("Pi"), 11, None, SHR)
        TS(R("XYi", 8, 16), R("Pi"), 2047, None, AND)

        def pass_names():
            TC(R("XYs"), R("XYi"))
            remote(t, "n", "XY%d" % (t + 1), R("XYs"))

        def pass_needs():
            TT(R("kj"), R("k0"), R("KJ"), A.mult)
            TS(R("FC3"), R("QC", 16, 24), 5, W - 1, SHR, AND)
            TT(R("far2"), R("FC3"), R("kj"), A.max)
            TC(R("farU"), R("far2"))
            TS(R("Zs"), IND(R("MW"), R("farU")), 0.5, 127.75, A.mult, A.add)
            remote(t, "z", "Z%d" % (t + 1), R("Zs"))
        if t < ROUNDS - 1:
            pass_names()
        TS(R("UWN", 0, 8), R("XYi", 0, 8), 2.0, 17.0, A.mult, A.add)
        TS(R("UWN", 8, 16), R("XYi", 8, 16), 2.0, 593.0, A.mult, A.add)
        TT(R("QC", 16, 24), R("UWN", 0, 8), R("UWN", 8, 16), A.mult)
        if t < ROUNDS - 1:
            pass_needs()
        TT(R("QC", 0, 8), R("UWO", 0, 8), R("UWN", 8, 16), A.mult)
        TT(R("QC", 8, 16), R("UWN", 0, 8), R("UWO", 8, 16), A.mult)
        TS(R("gn"), R("k0"), 0.0, 64.0, eq, A.mult)
        TS(R("HLi", 0, 24), R("QC"), 13, 15, SHR, AND)
        TS(R("HLi", 24, 48), R("QC"), 5, 255, SHR, AND)
        TC(R("HLf"), R("HLi"))
        suppress(NS[t])
        if t == ROUNDS - 1:
            pass_names()
            pass_needs()
            TT(R("SG"), X(T.HLC[:, 0, :], "HLC", 0, 256), R("pH", 0, 256), A.subtract)
            TS(R("SG"), R("SG"), 0.0, 2.0, A.is_gt, A.mult)
            TS(R("SG"), R("SG"), -1.0, None, A.add)

    e = ROUNDS
    banks = ("pA", "pB", "pJP", "pM")
    for k in range(8):
        nm = banks[k % 4]
        for x in range(2):
            MM(R(nm, 256 * x, 256 * x + 256), [(X(T.EXPM[:, 2 * k + x, :], "EXPM"), R("SG"))])
        TT(R("YF", 512 * k, 512 * k + 512), R("MW", 512 * k, 512 * k + 512), R(nm, 0, 512), A.mult)
        if k == 0:
            dma("s", (T.yf[:, 0:512 - ROT], EXT), R("YF", ROT, 512))
            dma("y", (T.yf[:, W - ROT:W], EXT), R("YF", 0, ROT))
            TT(R("cst"), R("cf"), R("G"), A.mult)
            TS(R("cst"), R("cst"), -1.0, None, A.add)
            for x in range(ROUNDS):
                dma(("s", "y")[x % 2], (T.yc[:, 128 * x:128 * x + 128], EXT), R("cst", 8 * x, 8 * x + 8))
        elif k % 2 == 0:
            dma(("s", "y")[k // 2 % 2], (T.yf[:, 512 * (k - 1) - ROT:512 * (k + 1) - ROT], EXT), R("YF", 512 * (k - 1), 512 * (k + 1)))
        if k == 5:
            TC(R("YP"), R("XY%d" % e))
            dma("y", (T.yp[:], EXT), R("YP"))
    dma("s", (T.yf[:, 3584 - ROT:W - ROT], EXT), R("YF", 3584, W))
    TS(R("YZ"), R("Z%d" % e), -128.0, None, A.add)
    dma("y", (T.yz[:], EXT), R("YZ"))
    for s, n in sorted(count.items()):
        if known["g"].get(s, 0) < n:
            g.wait_ge(T.sem[s], n)
